import numpy as np
import ml_dtypes


def mxq(x, axis, fmt="e4m3"):
    dtype, down = {"e4m3": (ml_dtypes.float8_e4m3fn, 7), "e5m2": (ml_dtypes.float8_e5m2, 14)}[fmt]
    v = np.moveaxis(np.asarray(x, np.float32).astype(ml_dtypes.bfloat16).astype(np.float64), axis, -1)
    blocks = v.reshape(v.shape[:-1] + (-1, 32))
    amax = np.abs(blocks).max(-1, keepdims=True)
    byte = np.maximum(np.where(amax > 0, np.frexp(amax)[1] - 1 + 127, 0) - down, 1)
    scale = np.exp2(byte - 127.0)
    codes = (blocks / scale).astype(np.float32).astype(dtype).astype(np.float64)
    return np.moveaxis((codes * scale).reshape(v.shape), -1, axis)


WIDE = False


def mx_kscale(k):
    if not WIDE:
        return np.ones(k)
    levels = np.array([10, -10, 5, -5, 0])
    if k % 512:
        return np.exp2(np.random.permutation(np.resize(levels, k // 32))).repeat(32)
    a = np.empty((k // 512, 16))
    for p in range(k // 512):
        a[p, :8] = np.random.permutation(np.resize(levels, 8))
        for g in range(8):
            far = levels[np.abs(levels - a[p, g]) >= 10]
            a[p, g + 8] = far[np.random.randint(len(far))]
    return np.exp2(a.ravel()).repeat(32)


def f64(x):
    return np.asarray(x).astype(np.float64)


def striped(idx):
    return np.tile(idx.reshape(-1, 16).T, (8, 1)).astype(np.uint16)


def unstriped(offs):
    return offs[:16].T.reshape(-1).astype(np.int64)


E2M1 = np.array([0.0, 0.5, 1.0, 1.5, 2.0, 3.0, 4.0, 6.0, -0.0, -0.5, -1.0, -1.5, -2.0, -3.0, -4.0, -6.0])


def pack_weight(w, fmt):
    k, n = w.shape
    w = f64(np.asarray(w, np.float32).astype(ml_dtypes.bfloat16)).reshape(k // 32, 32, n)
    amax = np.abs(w).max(1)
    if fmt == "e4m3":
        byte = np.frexp(amax)[1] - 1 + 127 - 7
    else:
        mant, ex = np.frexp(amax / 6.0)
        byte = np.where(mant > 0.5, ex, ex - 1) + 127
    byte = np.clip(np.where(amax > 0, byte, 1), 1, 254)
    scaled = (w * np.exp2(127.0 - byte)[:, None, :]).reshape(k, n).astype(np.float32)
    by_word = np.ascontiguousarray(scaled.reshape(k // 512, 128, 4, n).transpose(0, 1, 3, 2))
    if fmt == "e4m3":
        words = by_word.astype(ml_dtypes.float8_e4m3fn).view(np.uint8)
    else:
        c = by_word.astype(ml_dtypes.float4_e2m1fn).view(np.uint8) & 0xF
        words = (c[..., 0::2] | (c[..., 1::2] << 4)).reshape(k // 512, 128, 2 * n)
    return np.ascontiguousarray(words), np.ascontiguousarray(byte.astype(np.uint8).reshape(k // 512, 16, n))


def unpack_weight(words, scales, fmt):
    g, _, n = scales.shape
    words = np.ascontiguousarray(words).reshape(g, 128, n, -1)
    if fmt == "e4m3":
        vals = words.view(ml_dtypes.float8_e4m3fn).astype(np.float64)
    else:
        nib = np.empty((g, 128, n, 4), np.uint8)
        nib[..., 0::2] = words & 0xF
        nib[..., 1::2] = words >> 4
        vals = E2M1[nib]
    vals = vals * np.repeat(np.exp2(scales.astype(np.float64) - 127.0), 8, axis=1)[..., None]
    return vals.transpose(0, 1, 3, 2).reshape(g * 512, n)


def silu(v):
    return v / (1.0 + np.exp(-np.maximum(v, -700.0)))


K, T, E, C, N = 1536, 640, 15, 128, 128
TOP = 3


def by_expert(wq, xq):
    return np.concatenate([wq[e].T @ xq[:, e * C:(e + 1) * C] for e in range(E)], axis=1)


def setup_inputs():
    n = np.random.standard_normal
    s = mx_kscale(K)[:, None]
    deal = np.repeat(np.arange(E), C).reshape(TOP, T)[:, np.random.permutation(T)]
    deal = np.take_along_axis(deal, np.argsort(np.random.rand(TOP, T), axis=0), axis=0)
    for _ in range(8):
        s_, t_ = np.random.permutation(T).reshape(2, -1); r = np.random.randint(TOP, size=T // 2); x, y = deal[r, s_].copy(), deal[r, t_].copy()
        ok = ~((deal[:, s_] == y).any(0) | (deal[:, t_] == x).any(0)); deal[r[ok], s_[ok]] = y[ok]; deal[r[ok], t_[ok]] = x[ok]
    order = np.lexsort((np.random.rand(TOP * T), deal.reshape(-1)))
    slot_token = order % T; pos = np.empty(TOP * T, np.int64); pos[order] = np.arange(TOP * T); pos = pos.reshape(TOP, T)
    g = np.random.uniform(0.5, 1.5, (TOP, T)); g = g / g.sum(0)
    w = [pack_weight(m, "e2m1") for m in n((E, K, N)) / np.sqrt(K) / s[None]]
    return {
        "xT": (n((K, T)) * s).astype(np.float32),
        "w_words": np.stack([m[0] for m in w]),
        "w_scales": np.stack([m[1] for m in w]),
        "b": (0.3 * n((N, E))).astype(np.float32),
        "gate": np.stack([np.tile(r, (N, 1)) for r in g]).astype(np.float32),
        "offs": striped(slot_token),
        "pos1": striped(pos[0]),
        "pos2": striped(pos[1]),
        "pos3": striped(pos[2]),
    }


def reference(xT, w_words, w_scales, b, gate, offs, pos1, pos2, pos3):
    idx = unstriped(offs)
    w = np.stack([unpack_weight(w_words[e], w_scales[e], "e2m1") for e in range(E)])
    xq = mxq(f64(xT)[:, idx], 0, "e4m3")
    y = by_expert(w, xq)
    y = silu(y + np.repeat(f64(b), C, axis=1))
    return sum(f64(gate[r]) * y[:, unstriped(p)] for r, p in enumerate((pos1, pos2, pos3)))

@@ -1,0 +1,176 @@
+from contextlib import ExitStack
+
+import concourse.mybir as mybir
+
+K, T, E, C, N = 1536, 640, 15, 128, 128
+TOP = 3
+FLOPS = 2 * K * N * E * C
+
+P = 128
+PACK = 4
+A = 3
+S = E * C
+
+F32 = mybir.dt.float32
+BF16 = mybir.dt.bfloat16
+U32 = mybir.dt.uint32
+I32 = mybir.dt.int32
+U16 = mybir.dt.uint16
+U8 = mybir.dt.uint8
+FP8X4 = mybir.dt.float8_e4m3fn_x4
+FP4X4 = mybir.dt.float4_e2m1fn_x4
+COPY = mybir.ActivationFunctionType.Copy
+SILU = mybir.ActivationFunctionType.Silu
+ADD = mybir.AluOpType.add
+MULT = mybir.AluOpType.mult
+
+
+def interleaved_views(dst, src):
+    return dst.rearrange("p (c i) j -> p c j i", i=4), src.rearrange("p j (c i) -> p c j i", i=4)
+
+
+def tile_moe_tk_lin_silu_kernel(
+    tc, xT, w_words, w_scales, b, gate, offs, pos1, pos2, pos3, out
+):
+    nc = tc.nc
+    with ExitStack() as ctx:
+        keep = ctx.enter_context(tc.tile_pool(name="keep", bufs=1))
+        psum = ctx.enter_context(tc.psum_pool(name="psum", bufs=8))
+
+        offs_sb = keep.tile([P, S // 16], U16, name="offs_sb")
+        pos_sb = [keep.tile([P, T // 16], U16, name=f"pos{r}_sb") for r in range(TOP)]
+        x_cuts = [[0, 256, 512, 640], [0, 320, 640], [0, 320, 640]]
+        x_sb = [
+            [keep.tile([P, PACK, hi - lo], F32, name=f"x{a}_{lo}") for lo, hi in zip(x_cuts[a], x_cuts[a][1:])]
+            for a in range(A)
+        ]
+        xb = [keep.tile([P, T, PACK], BF16, name=f"xb{a}", align_bytes=64) for a in range(A)]
+        words = [keep.tile([P, T], U32, name=f"words{a}", align_bytes=64) for a in range(A)]
+        bytes3 = keep.tile([P, T], U8, name="bytes3", align_bytes=64)
+        gwords = [keep.tile([P, S], U32, name=f"gwords{a}", align_bytes=64) for a in range(A)]
+        gbytes = [keep.tile([P, S], U8, name=f"gbytes{a}", align_bytes=64) for a in range(A)]
+        w_sb = keep.tile([P, E * A, 2 * N], U8, name="w_sb", align_bytes=64)
+        ws_sb = keep.tile([P, E * A, N], U8, name="ws_sb", align_bytes=64)
+        b_sb = keep.tile([P, E], F32, name="b_sb")
+        gate_sb = keep.tile([P, TOP, T], F32, name="gate_sb")
+        y_sb = keep.tile([P, S], F32, name="y_sb")
+        prod = [keep.tile([P, T], F32, name=f"prod{r}") for r in range(TOP)]
+        part = keep.tile([P, T], F32, name="part")
+        o_sb = keep.tile([P, T], F32, name="o_sb")
+        warm = keep.tile([P, 1], F32, name="warm")
+        warm_out = keep.tile([P, 1], F32, name="warm_out")
+
+        nc.vector.memset(warm[:], 0.0)
+        nc.scalar.activation(warm_out[:], warm[:], SILU)
+        nc.gpsimd.memset(bytes3[:], 0)
+        nc.gpsimd.memset(ws_sb[:].rearrange("p i n -> p (i n)").bitcast(I32), 0)
+        nc.gpsimd.memset(gbytes[1][:].bitcast(I32), 0)
+        nc.gpsimd.memset(gbytes[2][:].bitcast(I32), 0)
+
+        for a in range(A):
+            rows = xT[a * 512 : (a + 1) * 512, :].rearrange("(p j) t -> p j t", j=PACK)
+            for i, (lo, hi) in enumerate(zip(x_cuts[a], x_cuts[a][1:])):
+                nc.sync.dma_start(out=x_sb[a][i][:], in_=rows[:, :, lo:hi])
+            if a == 0:
+                nc.sync.dma_start(offs_sb[:], offs)
+        for q in range(4):
+            nc.sync.dma_start(
+                out=ws_sb[32 * q : 32 * q + 4].bitcast(I32),
+                in_=w_scales[:, :, 4 * q : 4 * q + 4, :].rearrange("e a q n -> q (e a) n").bitcast(I32),
+            )
+        nc.sync.dma_start(b_sb[:], b)
+        for e0 in range(0, E, 5):
+            nc.sync.dma_start(
+                out=w_sb[:, e0 * A : (e0 + 5) * A, :].bitcast(I32),
+                in_=w_words[e0 : e0 + 5].rearrange("e a p c -> p (e a) c").bitcast(I32),
+            )
+        for r, lst in enumerate((pos1, pos2, pos3)):
+            nc.sync.dma_start(pos_sb[r][:], lst)
+        nc.sync.dma_start(gate_sb[:], gate.rearrange("r p t -> p r t"))
+
+        def interleave(a, i, vector_columns):
+            lo, hi = x_cuts[a][i], x_cuts[a][i + 1]
+            mid = lo + vector_columns
+            if mid > lo:
+                dst, src = interleaved_views(xb[a][:, lo:mid, :], x_sb[a][i][:, :, 0 : mid - lo])
+                nc.vector.tensor_copy(dst, src)
+            dst, src = interleaved_views(xb[a][:, mid:hi, :], x_sb[a][i][:, :, mid - lo : hi - lo])
+            nc.scalar.activation(dst, src, COPY)
+
+        def quantize(a, lo, hi):
+            nc.vector.quantize_mx(
+                out=words[a][:, lo:hi].bitcast(FP8X4),
+                scales=bytes3[4 * a :, lo:hi],
+                in_=xb[a][:, lo:hi, :].rearrange("p t j -> p (t j)"),
+            )
+
+        def gather_words(a, lo, hi):
+            nc.vector.tensor_copy(gwords[a][:, lo:hi], words[a][:].indirect(offs_sb[:, lo // 16 : hi // 16]))
+
+        def gather_bytes(lo, hi):
+            nc.vector.tensor_copy(gbytes[0][:, lo:hi], bytes3[:].indirect(offs_sb[:, lo // 16 : hi // 16]))
+
+        def shift_bytes(lo, hi):
+            for a in (1, 2):
+                nc.sync.dma_start(
+                    out=gbytes[a][0:112, lo:hi].bitcast(I32), in_=gbytes[0][4 * a : 4 * a + 112, lo:hi].bitcast(I32)
+                )
+
+        def expert(e):
+            cols = slice(e * C, (e + 1) * C)
+            acc = psum.tile([P, C], F32, name="acc")
+            for a in range(A):
+                i = e * A + a
+                nc.tensor.matmul_mx(
+                    out=acc[:],
+                    lhsT=w_sb[:, i, :].bitcast(FP4X4),
+                    lhsT_scale=ws_sb[:, i, :],
+                    rhs=gwords[a][:, cols].bitcast(FP8X4),
+                    rhs_scale=gbytes[a][:, cols],
+                    start=(a == 0),
+                    stop=(a == A - 1),
+                )
+            nc.scalar.activation(y_sb[:, cols], acc[:], SILU, bias=b_sb[:, e : e + 1])
+
+        interleave(0, 0, 176)
+        interleave(0, 1, 176)
+        quantize(0, 0, 256)
+        interleave(0, 2, 80)
+        quantize(0, 256, 512)
+        quantize(0, 512, 640)
+        for i in range(2):
+            interleave(1, i, 0)
+        for i in range(2):
+            interleave(2, i, 0)
+        chunks = [(0, 480), (480, 960), (960, 1440), (1440, 1920)]
+        for lo, hi in chunks:
+            gather_words(0, lo, hi)
+        quantize(1, 0, 512)
+        quantize(1, 512, 640)
+        for lo, hi in chunks[:2]:
+            gather_words(1, lo, hi)
+        quantize(2, 0, 512)
+        quantize(2, 512, 640)
+        for lo, hi in chunks[:2]:
+            gather_bytes(lo, hi)
+        shift_bytes(0, 960)
+        for lo, hi in chunks[2:]:
+            gather_bytes(lo, hi)
+        shift_bytes(960, 1920)
+        done = 0
+        for c, (lo, hi) in enumerate([(0, 384), (384, 768), (768, 1152), (1152, 1536), (1536, 1792), (1792, 1920)]):
+            if hi > 960:
+                gather_words(1, max(lo, 960), hi)
+            gather_words(2, lo, hi)
+            for e in range(lo // C, hi // C):
+                expert(e)
+
+        for t0 in range(0, T, 320):
+            ts = slice(t0, t0 + 320)
+            for r in range(TOP):
+                nc.vector.tensor_tensor(
+                    prod[r][:, ts], y_sb[:].indirect(pos_sb[r][:, t0 // 16 : (t0 + 320) // 16]), gate_sb[:, r, ts], MULT
+                )
+            nc.vector.tensor_tensor(part[:, ts], prod[0][:, ts], prod[1][:, ts], ADD)
+            nc.vector.tensor_tensor(o_sb[:, ts], part[:, ts], prod[2][:, ts], ADD)
+            nc.sync.dma_start(out[:, ts], o_sb[:, ts])

@@ -10,6 +10,7 @@ P = 128
 PACK = 4
 A = 3
 S = E * C
+WIN = 2048
 
 F32 = mybir.dt.float32
 BF16 = mybir.dt.bfloat16
@@ -39,20 +40,19 @@ def tile_moe_tk_lin_silu_kernel(
 
         offs_sb = keep.tile([P, S // 16], U16, name="offs_sb")
         pos_sb = [keep.tile([P, T // 16], U16, name=f"pos{r}_sb") for r in range(TOP)]
-        x_cuts = [[0, 256, 512, 640], [0, 320, 640], [0, 320, 640]]
+        x_cuts = [[0, 384, 640], [0, 320, 640], [0, 320, 640]]
         x_sb = [
             [keep.tile([P, PACK, hi - lo], F32, name=f"x{a}_{lo}") for lo, hi in zip(x_cuts[a], x_cuts[a][1:])]
             for a in range(A)
         ]
         xb = [keep.tile([P, T, PACK], BF16, name=f"xb{a}", align_bytes=64) for a in range(A)]
-        words = [keep.tile([P, T], U32, name=f"words{a}", align_bytes=64) for a in range(A)]
-        bytes3 = keep.tile([P, T], U8, name="bytes3", align_bytes=64)
+        words = [keep.tile([P, WIN], U32, name=f"words{a}", align_bytes=64) for a in range(A)]
+        bytes3 = keep.tile([P, WIN], U8, name="bytes3", tag="late", align_bytes=64)
         gwords = [keep.tile([P, S], U32, name=f"gwords{a}", align_bytes=64) for a in range(A)]
         gbytes = [keep.tile([P, S], U8, name=f"gbytes{a}", align_bytes=64) for a in range(A)]
         w_sb = keep.tile([P, E * A, 2 * N], U8, name="w_sb", align_bytes=64)
         ws_sb = keep.tile([P, E * A, N], U8, name="ws_sb", align_bytes=64)
         b_sb = keep.tile([P, E], F32, name="b_sb")
-        gate_sb = keep.tile([P, TOP, T], F32, name="gate_sb")
         y_sb = keep.tile([P, S], F32, name="y_sb")
         prod = [keep.tile([P, T], F32, name=f"prod{r}") for r in range(TOP)]
         part = keep.tile([P, T], F32, name="part")
@@ -62,8 +62,8 @@ def tile_moe_tk_lin_silu_kernel(
 
         nc.vector.memset(warm[:], 0.0)
         nc.scalar.activation(warm_out[:], warm[:], SILU)
-        nc.gpsimd.memset(bytes3[:], 0)
-        nc.gpsimd.memset(ws_sb[:].rearrange("p i n -> p (i n)").bitcast(I32), 0)
+        nc.gpsimd.memset(bytes3[:, 0:T], 0)
+        nc.vector.memset(ws_sb[:].rearrange("p i n -> p (i n)").bitcast(I32), 0)
         nc.gpsimd.memset(gbytes[1][:].bitcast(I32), 0)
         nc.gpsimd.memset(gbytes[2][:].bitcast(I32), 0)
 
@@ -73,20 +73,23 @@ def tile_moe_tk_lin_silu_kernel(
                 nc.sync.dma_start(out=x_sb[a][i][:], in_=rows[:, :, lo:hi])
             if a == 0:
                 nc.sync.dma_start(offs_sb[:], offs)
+            if a == 1:
+                nc.sync.dma_start(b_sb[:], b)
         for q in range(4):
             nc.sync.dma_start(
                 out=ws_sb[32 * q : 32 * q + 4].bitcast(I32),
                 in_=w_scales[:, :, 4 * q : 4 * q + 4, :].rearrange("e a q n -> q (e a) n").bitcast(I32),
             )
-        nc.sync.dma_start(b_sb[:], b)
-        for e0 in range(0, E, 5):
+        for e0, e1 in ((0, 8), (8, E)):
             nc.sync.dma_start(
-                out=w_sb[:, e0 * A : (e0 + 5) * A, :].bitcast(I32),
-                in_=w_words[e0 : e0 + 5].rearrange("e a p c -> p (e a) c").bitcast(I32),
+                out=w_sb[:, e0 * A : e1 * A, :].bitcast(I32),
+                in_=w_words[e0:e1].rearrange("e a p c -> p (e a) c").bitcast(I32),
             )
         for r, lst in enumerate((pos1, pos2, pos3)):
             nc.sync.dma_start(pos_sb[r][:], lst)
-        nc.sync.dma_start(gate_sb[:], gate.rearrange("r p t -> p r t"))
+
+        def window(n):
+            return WIN if n >= 256 else T
 
         def interleave(a, i, vector_columns):
             lo, hi = x_cuts[a][i], x_cuts[a][i + 1]
@@ -94,8 +97,10 @@ def tile_moe_tk_lin_silu_kernel(
             if mid > lo:
                 dst, src = interleaved_views(xb[a][:, lo:mid, :], x_sb[a][i][:, :, 0 : mid - lo])
                 nc.vector.tensor_copy(dst, src)
-            dst, src = interleaved_views(xb[a][:, mid:hi, :], x_sb[a][i][:, :, mid - lo : hi - lo])
-            nc.scalar.activation(dst, src, COPY)
+            for c0 in range(mid, hi, 320):
+                c1 = min(c0 + 320, hi)
+                dst, src = interleaved_views(xb[a][:, c0:c1, :], x_sb[a][i][:, :, c0 - lo : c1 - lo])
+                nc.scalar.activation(dst, src, COPY)
 
         def quantize(a, lo, hi):
             nc.vector.quantize_mx(
@@ -105,14 +110,14 @@ def tile_moe_tk_lin_silu_kernel(
             )
 
         def gather_words(a, lo, hi):
-            nc.vector.tensor_copy(gwords[a][:, lo:hi], words[a][:].indirect(offs_sb[:, lo // 16 : hi // 16]))
+            nc.vector.tensor_copy(gwords[a][:, lo:hi], words[a][:, 0 : window(hi - lo)].indirect(offs_sb[:, lo // 16 : hi // 16]))
 
         def gather_bytes(lo, hi):
-            nc.vector.tensor_copy(gbytes[0][:, lo:hi], bytes3[:].indirect(offs_sb[:, lo // 16 : hi // 16]))
+            nc.vector.tensor_copy(gbytes[0][:, lo:hi], bytes3[:, 0 : window(hi - lo)].indirect(offs_sb[:, lo // 16 : hi // 16]))
 
         def shift_bytes(lo, hi):
             for a in (1, 2):
-                nc.sync.dma_start(
+                nc.scalar.dma_start(
                     out=gbytes[a][0:112, lo:hi].bitcast(I32), in_=gbytes[0][4 * a : 4 * a + 112, lo:hi].bitcast(I32)
                 )
 
@@ -132,45 +137,40 @@ def tile_moe_tk_lin_silu_kernel(
                 )
             nc.scalar.activation(y_sb[:, cols], acc[:], SILU, bias=b_sb[:, e : e + 1])
 
-        interleave(0, 0, 176)
-        interleave(0, 1, 176)
+        interleave(0, 0, 256)
         quantize(0, 0, 256)
-        interleave(0, 2, 80)
-        quantize(0, 256, 512)
-        quantize(0, 512, 640)
+        interleave(0, 1, 176)
+        quantize(0, 256, 384)
+        quantize(0, 384, 640)
         for i in range(2):
             interleave(1, i, 0)
         for i in range(2):
             interleave(2, i, 0)
-        chunks = [(0, 480), (480, 960), (960, 1440), (1440, 1920)]
-        for lo, hi in chunks:
-            gather_words(0, lo, hi)
+        gather_words(0, 0, 1536)
+        gather_words(0, 1536, S)
         quantize(1, 0, 512)
         quantize(1, 512, 640)
-        for lo, hi in chunks[:2]:
-            gather_words(1, lo, hi)
+        gather_words(1, 0, 1152)
         quantize(2, 0, 512)
         quantize(2, 512, 640)
-        for lo, hi in chunks[:2]:
-            gather_bytes(lo, hi)
+        gather_bytes(0, 960)
         shift_bytes(0, 960)
-        for lo, hi in chunks[2:]:
-            gather_bytes(lo, hi)
+        gather_bytes(960, 1920)
         shift_bytes(960, 1920)
-        done = 0
-        for c, (lo, hi) in enumerate([(0, 384), (384, 768), (768, 1152), (1152, 1536), (1536, 1792), (1792, 1920)]):
-            if hi > 960:
-                gather_words(1, max(lo, 960), hi)
+        gate_sb = keep.tile([P, TOP, T], F32, name="gate_sb", tag="late", align_bytes=64)
+        nc.sync.dma_start(gate_sb[:], gate.rearrange("r p t -> p r t"))
+        for lo, hi in [(0, 384), (384, 768), (768, 1152), (1152, 1536), (1536, 1792), (1792, 1920)]:
+            if lo in (1152, 1536):
+                gather_words(1, lo, lo + 384)
             gather_words(2, lo, hi)
             for e in range(lo // C, hi // C):
                 expert(e)
 
-        for t0 in range(0, T, 320):
-            ts = slice(t0, t0 + 320)
-            for r in range(TOP):
-                nc.vector.tensor_tensor(
-                    prod[r][:, ts], y_sb[:].indirect(pos_sb[r][:, t0 // 16 : (t0 + 320) // 16]), gate_sb[:, r, ts], MULT
-                )
+        for r in range(TOP):
+            nc.vector.tensor_tensor(prod[r][:], y_sb[:].indirect(pos_sb[r][:]), gate_sb[:, r, :], MULT)
+        halves = (slice(0, 320), slice(320, 640))
+        for ts in halves:
             nc.vector.tensor_tensor(part[:, ts], prod[0][:, ts], prod[1][:, ts], ADD)
+        for ts in halves:
             nc.vector.tensor_tensor(o_sb[:, ts], part[:, ts], prod[2][:, ts], ADD)
             nc.sync.dma_start(out[:, ts], o_sb[:, ts])

from contextlib import ExitStack

import concourse.mybir as mybir

K, T, E, C, N = 1536, 640, 15, 128, 128
TOP = 3
FLOPS = 2 * K * N * E * C

P = 128
PACK = 4
A = 3
S = E * C
WIN = 2048

F32 = mybir.dt.float32
BF16 = mybir.dt.bfloat16
U32 = mybir.dt.uint32
I32 = mybir.dt.int32
U16 = mybir.dt.uint16
U8 = mybir.dt.uint8
FP8X4 = mybir.dt.float8_e4m3fn_x4
FP4X4 = mybir.dt.float4_e2m1fn_x4
COPY = mybir.ActivationFunctionType.Copy
SILU = mybir.ActivationFunctionType.Silu
ADD = mybir.AluOpType.add
MULT = mybir.AluOpType.mult


def interleaved_views(dst, src):
    return dst.rearrange("p (c i) j -> p c j i", i=4), src.rearrange("p j (c i) -> p c j i", i=4)


def tile_moe_tk_lin_silu_kernel(
    tc, xT, w_words, w_scales, b, gate, offs, pos1, pos2, pos3, out
):
    nc = tc.nc
    with ExitStack() as ctx:
        keep = ctx.enter_context(tc.tile_pool(name="keep", bufs=1))
        psum = ctx.enter_context(tc.psum_pool(name="psum", bufs=8))

        offs_sb = keep.tile([P, S // 16], U16, name="offs_sb")
        pos_sb = [keep.tile([P, T // 16], U16, name=f"pos{r}_sb") for r in range(TOP)]
        x_cuts = [[0, 384, 640], [0, 320, 640], [0, 320, 640]]
        x_sb = [
            [keep.tile([P, PACK, hi - lo], F32, name=f"x{a}_{lo}") for lo, hi in zip(x_cuts[a], x_cuts[a][1:])]
            for a in range(A)
        ]
        xb = [keep.tile([P, T, PACK], BF16, name=f"xb{a}", align_bytes=64) for a in range(A)]
        words = [keep.tile([P, WIN], U32, name=f"words{a}", align_bytes=64) for a in range(A)]
        bytes3 = keep.tile([P, WIN], U8, name="bytes3", tag="late", align_bytes=64)
        gwords = [keep.tile([P, S], U32, name=f"gwords{a}", align_bytes=64) for a in range(A)]
        gbytes = [keep.tile([P, S], U8, name=f"gbytes{a}", align_bytes=64) for a in range(A)]
        w_sb = keep.tile([P, E * A, 2 * N], U8, name="w_sb", align_bytes=64)
        ws_sb = keep.tile([P, E * A, N], U8, name="ws_sb", align_bytes=64)
        b_sb = keep.tile([P, E], F32, name="b_sb")
        y_sb = keep.tile([P, S], F32, name="y_sb")
        prod = [keep.tile([P, T], F32, name=f"prod{r}") for r in range(TOP)]
        part = keep.tile([P, T], F32, name="part")
        o_sb = keep.tile([P, T], F32, name="o_sb")
        warm = keep.tile([P, 1], F32, name="warm")
        warm_out = keep.tile([P, 1], F32, name="warm_out")

        nc.vector.memset(warm[:], 0.0)
        nc.scalar.activation(warm_out[:], warm[:], SILU)
        nc.gpsimd.memset(bytes3[:, 0:T], 0)
        nc.vector.memset(ws_sb[:].rearrange("p i n -> p (i n)").bitcast(I32), 0)
        nc.gpsimd.memset(gbytes[1][:].bitcast(I32), 0)
        nc.gpsimd.memset(gbytes[2][:].bitcast(I32), 0)

        for a in range(A):
            rows = xT[a * 512 : (a + 1) * 512, :].rearrange("(p j) t -> p j t", j=PACK)
            for i, (lo, hi) in enumerate(zip(x_cuts[a], x_cuts[a][1:])):
                nc.sync.dma_start(out=x_sb[a][i][:], in_=rows[:, :, lo:hi])
            if a == 0:
                nc.sync.dma_start(offs_sb[:], offs)
            if a == 1:
                nc.sync.dma_start(b_sb[:], b)
        for q in range(4):
            nc.sync.dma_start(
                out=ws_sb[32 * q : 32 * q + 4].bitcast(I32),
                in_=w_scales[:, :, 4 * q : 4 * q + 4, :].rearrange("e a q n -> q (e a) n").bitcast(I32),
            )
        for e0, e1 in ((0, 8), (8, E)):
            nc.sync.dma_start(
                out=w_sb[:, e0 * A : e1 * A, :].bitcast(I32),
                in_=w_words[e0:e1].rearrange("e a p c -> p (e a) c").bitcast(I32),
            )
        for r, lst in enumerate((pos1, pos2, pos3)):
            nc.sync.dma_start(pos_sb[r][:], lst)

        def window(n):
            return WIN if n >= 256 else T

        def interleave(a, i, vector_columns):
            lo, hi = x_cuts[a][i], x_cuts[a][i + 1]
            mid = lo + vector_columns
            if mid > lo:
                dst, src = interleaved_views(xb[a][:, lo:mid, :], x_sb[a][i][:, :, 0 : mid - lo])
                nc.vector.tensor_copy(dst, src)
            for c0 in range(mid, hi, 320):
                c1 = min(c0 + 320, hi)
                dst, src = interleaved_views(xb[a][:, c0:c1, :], x_sb[a][i][:, :, c0 - lo : c1 - lo])
                nc.scalar.activation(dst, src, COPY)

        def quantize(a, lo, hi):
            nc.vector.quantize_mx(
                out=words[a][:, lo:hi].bitcast(FP8X4),
                scales=bytes3[4 * a :, lo:hi],
                in_=xb[a][:, lo:hi, :].rearrange("p t j -> p (t j)"),
            )

        def gather_words(a, lo, hi):
            nc.vector.tensor_copy(gwords[a][:, lo:hi], words[a][:, 0 : window(hi - lo)].indirect(offs_sb[:, lo // 16 : hi // 16]))

        def gather_bytes(lo, hi):
            nc.vector.tensor_copy(gbytes[0][:, lo:hi], bytes3[:, 0 : window(hi - lo)].indirect(offs_sb[:, lo // 16 : hi // 16]))

        def shift_bytes(lo, hi):
            for a in (1, 2):
                nc.scalar.dma_start(
                    out=gbytes[a][0:112, lo:hi].bitcast(I32), in_=gbytes[0][4 * a : 4 * a + 112, lo:hi].bitcast(I32)
                )

        def expert(e):
            cols = slice(e * C, (e + 1) * C)
            acc = psum.tile([P, C], F32, name="acc")
            for a in range(A):
                i = e * A + a
                nc.tensor.matmul_mx(
                    out=acc[:],
                    lhsT=w_sb[:, i, :].bitcast(FP4X4),
                    lhsT_scale=ws_sb[:, i, :],
                    rhs=gwords[a][:, cols].bitcast(FP8X4),
                    rhs_scale=gbytes[a][:, cols],
                    start=(a == 0),
                    stop=(a == A - 1),
                )
            nc.scalar.activation(y_sb[:, cols], acc[:], SILU, bias=b_sb[:, e : e + 1])

        interleave(0, 0, 256)
        quantize(0, 0, 256)
        interleave(0, 1, 176)
        quantize(0, 256, 384)
        quantize(0, 384, 640)
        for i in range(2):
            interleave(1, i, 0)
        for i in range(2):
            interleave(2, i, 0)
        gather_words(0, 0, 1536)
        gather_words(0, 1536, S)
        quantize(1, 0, 512)
        quantize(1, 512, 640)
        gather_words(1, 0, 1152)
        quantize(2, 0, 512)
        quantize(2, 512, 640)
        gather_bytes(0, 960)
        shift_bytes(0, 960)
        gather_bytes(960, 1920)
        shift_bytes(960, 1920)
        gate_sb = keep.tile([P, TOP, T], F32, name="gate_sb", tag="late", align_bytes=64)
        nc.sync.dma_start(gate_sb[:], gate.rearrange("r p t -> p r t"))
        for lo, hi in [(0, 384), (384, 768), (768, 1152), (1152, 1536), (1536, 1792), (1792, 1920)]:
            if lo in (1152, 1536):
                gather_words(1, lo, lo + 384)
            gather_words(2, lo, hi)
            for e in range(lo // C, hi // C):
                expert(e)

        for r in range(TOP):
            nc.vector.tensor_tensor(prod[r][:], y_sb[:].indirect(pos_sb[r][:]), gate_sb[:, r, :], MULT)
        halves = (slice(0, 320), slice(320, 640))
        for ts in halves:
            nc.vector.tensor_tensor(part[:, ts], prod[0][:, ts], prod[1][:, ts], ADD)
        for ts in halves:
            nc.vector.tensor_tensor(o_sb[:, ts], part[:, ts], prod[2][:, ts], ADD)
            nc.sync.dma_start(out[:, ts], o_sb[:, ts])
